import numpy as np
import ml_dtypes


def mxq(x, axis, fmt="e4m3"):
    dtype, down = {"e4m3": (ml_dtypes.float8_e4m3fn, 7), "e5m2": (ml_dtypes.float8_e5m2, 14)}[fmt]
    v = np.moveaxis(np.asarray(x, np.float32).astype(ml_dtypes.bfloat16).astype(np.float64), axis, -1)
    blocks = v.reshape(v.shape[:-1] + (-1, 32))
    amax = np.abs(blocks).max(-1, keepdims=True)
    byte = np.maximum(np.where(amax > 0, np.frexp(amax)[1] - 1 + 127, 0) - down, 1)
    scale = np.exp2(byte - 127.0)
    codes = (blocks / scale).astype(np.float32).astype(dtype).astype(np.float64)
    return np.moveaxis((codes * scale).reshape(v.shape), -1, axis)


WIDE = False


def mx_kscale(k):
    if not WIDE:
        return np.ones(k)
    levels = np.array([10, -10, 5, -5, 0])
    if k % 512:
        return np.exp2(np.random.permutation(np.resize(levels, k // 32))).repeat(32)
    a = np.empty((k // 512, 16))
    for p in range(k // 512):
        a[p, :8] = np.random.permutation(np.resize(levels, 8))
        for g in range(8):
            far = levels[np.abs(levels - a[p, g]) >= 10]
            a[p, g + 8] = far[np.random.randint(len(far))]
    return np.exp2(a.ravel()).repeat(32)


def f64(x):
    return np.asarray(x).astype(np.float64)


E2M1 = np.array([0.0, 0.5, 1.0, 1.5, 2.0, 3.0, 4.0, 6.0, -0.0, -0.5, -1.0, -1.5, -2.0, -3.0, -4.0, -6.0])


def pack_weight(w, fmt):
    k, n = w.shape
    w = f64(np.asarray(w, np.float32).astype(ml_dtypes.bfloat16)).reshape(k // 32, 32, n)
    amax = np.abs(w).max(1)
    if fmt == "e4m3":
        byte = np.frexp(amax)[1] - 1 + 127 - 7
    else:
        mant, ex = np.frexp(amax / 6.0)
        byte = np.where(mant > 0.5, ex, ex - 1) + 127
    byte = np.clip(np.where(amax > 0, byte, 1), 1, 254)
    scaled = (w * np.exp2(127.0 - byte)[:, None, :]).reshape(k, n).astype(np.float32)
    by_word = np.ascontiguousarray(scaled.reshape(k // 512, 128, 4, n).transpose(0, 1, 3, 2))
    if fmt == "e4m3":
        words = by_word.astype(ml_dtypes.float8_e4m3fn).view(np.uint8)
    else:
        c = by_word.astype(ml_dtypes.float4_e2m1fn).view(np.uint8) & 0xF
        words = (c[..., 0::2] | (c[..., 1::2] << 4)).reshape(k // 512, 128, 2 * n)
    return np.ascontiguousarray(words), np.ascontiguousarray(byte.astype(np.uint8).reshape(k // 512, 16, n))


def unpack_weight(words, scales, fmt):
    g, _, n = scales.shape
    words = np.ascontiguousarray(words).reshape(g, 128, n, -1)
    if fmt == "e4m3":
        vals = words.view(ml_dtypes.float8_e4m3fn).astype(np.float64)
    else:
        nib = np.empty((g, 128, n, 4), np.uint8)
        nib[..., 0::2] = words & 0xF
        nib[..., 1::2] = words >> 4
        vals = E2M1[nib]
    vals = vals * np.repeat(np.exp2(scales.astype(np.float64) - 127.0), 8, axis=1)[..., None]
    return vals.transpose(0, 1, 3, 2).reshape(g * 512, n)


def silu(v):
    return v / (1.0 + np.exp(-np.maximum(v, -700.0)))


O, K, M, T = 1024, 2560, 1024, 512


def setup_inputs():
    n = np.random.standard_normal
    s = mx_kscale(K)[:, None]
    x = n((K, T)); x[:O] *= 6.0
    w = n((K, M)) / np.sqrt(K) / s; w[:O] /= 2.0
    p_x4 = pack_weight(x[O:] * s[O:], "e2m1")
    p_w4 = pack_weight(w[O:], "e2m1")
    return {
        "x8": (x[:O] * s[:O]).astype(np.float32),
        "w8": (w[:O]).astype(np.float32),
        "x4_words": p_x4[0],
        "x4_scales": p_x4[1],
        "w4_words": p_w4[0],
        "w4_scales": p_w4[1],
        "b": (0.3 * n(1024)).astype(np.float32),
    }


def reference(x8, w8, x4_words, x4_scales, w4_words, w4_scales, b):
    x8_ = mxq(f64(x8), 0, "e4m3")
    w8_ = mxq(f64(w8), 0, "e4m3")
    x4_ = unpack_weight(x4_words, x4_scales, "e2m1")
    w4_ = unpack_weight(w4_words, w4_scales, "e2m1")
    y = x8_.T @ w8_ + x4_.T @ w4_
    return silu(y + f64(b)[None, :])

@@ -1,0 +1,207 @@
+from contextlib import ExitStack
+
+import concourse.mybir as mybir
+from concourse.masks import make_identity
+
+F32 = mybir.dt.float32
+BF16 = mybir.dt.bfloat16
+I32 = mybir.dt.int32
+U32 = mybir.dt.uint32
+U8 = mybir.dt.uint8
+FP8X4 = mybir.dt.float8_e4m3fn_x4
+FP4X4 = mybir.dt.float4_e2m1fn_x4
+SILU = mybir.ActivationFunctionType.Silu
+
+P = 128
+PACK = 4
+K_PASS = P * PACK
+T, N = 512, 1024
+K8, K4 = 1024, 1536
+G8, G4 = K8 // K_PASS, K4 // K_PASS
+TT = T // P
+
+FLOPS = 2 * (K8 + K4) * T * N
+
+CHUNKS = [256,512,256]
+V_COLS = [[160,160],[320,320],[160,160]]
+PIECES = [[(0, 0)], [(0, 1)], [(1, 0), (2, 0)], [(1, 1)], [(2, 1)]]
+STORE_GROUPS = [[0],[1],[2]]
+
+
+def interleave(copy, grouped, raw, c0, c1):
+    copy(
+        out=grouped[:, c0:c1, :].rearrange("p (c i) j -> p c j i", i=4),
+        in_=raw[:, :, c0:c1].rearrange("p j (c i) -> p c j i", i=4),
+    )
+
+
+def tile_mix_atom_tm_silu_kernel(tc, x8, w8, x4_words, x4_scales, w4_words, w4_scales, b, out):
+    nc = tc.nc
+    with ExitStack() as ctx:
+        sb = ctx.enter_context(tc.tile_pool(name="sb", bufs=1))
+        psum = ctx.enter_context(tc.psum_pool(name="psum", bufs=2))
+        ctx.enter_context(tc.manual_schedule())
+
+        starts = [sum(CHUNKS[:c]) for c in range(len(CHUNKS))]
+
+        x_raw = [sb.tile([P, PACK, T], F32, name="x_raw%d" % g) for g in range(G8)]
+        x_grp = [sb.tile([P, T, PACK], BF16, name="x_grp%d" % g, align_bytes=64) for g in range(G8)]
+        x_cod = [sb.tile([P, T], U32, name="x_cod%d" % g, align_bytes=64) for g in range(G8)]
+        x_scl = [sb.tile([P, T], U8, name="x_scl%d" % g, align_bytes=64) for g in range(G8)]
+        w_src = {}
+        w_grp = [[sb.tile([P, CHUNKS[c], PACK], BF16, name="w_grp%d_%d" % (c, g), align_bytes=64) for g in range(G8)] for c in range(len(CHUNKS))]
+        w_cod = [[sb.tile([P, CHUNKS[c]], U32, name="w_cod%d_%d" % (c, g), align_bytes=64) for g in range(G8)] for c in range(len(CHUNKS))]
+        w_scl = [[sb.tile([P, CHUNKS[c]], U8, name="w_scl%d_%d" % (c, g), align_bytes=64) for g in range(G8)] for c in range(len(CHUNKS))]
+        x4w = sb.tile([P, G4, 2 * T], U8, name="x4w", align_bytes=64)
+        w4w = sb.tile([P, G4, 2 * N], U8, name="w4w", align_bytes=64)
+        x4s = sb.tile([P, G4, T], U8, name="x4s", align_bytes=64)
+        w4s = sb.tile([P, G4, N], U8, name="w4s", align_bytes=64)
+        b_col = sb.tile([P, N // P], F32, name="b_col")
+        ident = sb.tile([P, P], F32, name="ident")
+        bias = sb.tile([P, N], F32, name="bias")
+        junk = sb.tile([P, 1], F32, name="junk")
+        junk2 = sb.tile([P, 1], F32, name="junk2")
+
+        nc.vector.memset(x4s[:].rearrange("p a n -> p (a n)").bitcast(I32), 0)
+        nc.vector.memset(junk[:], 0.0)
+        nc.vector.memset(w4s[:].rearrange("p a n -> p (a n)").bitcast(I32), 0)
+
+        x8_v = x8.rearrange("(g p j) t -> g p j t", p=P, j=PACK)
+        w8_v = w8.rearrange("(g p j) n -> g p j n", p=P, j=PACK)
+        ws_v = w4_scales.rearrange("a (q r) n -> r q a n", r=4)
+        xs_v = x4_scales.rearrange("a (q r) n -> r q a n", r=4)
+
+        nc.gpsimd.dma_start(out=b_col[:], in_=b.rearrange("(p c) -> p c", p=P))
+        make_identity(nc, ident[:])
+        for r in range(4):
+            nc.scalar.dma_start(out=x4s[r:P:32, :, :].bitcast(I32), in_=xs_v[r].bitcast(I32))
+        for r in range(2):
+            nc.scalar.dma_start(out=w4s[r:P:32, :, :].bitcast(I32), in_=ws_v[r].bitcast(I32))
+        for r in range(2, 4):
+            nc.gpsimd.dma_start(out=w4s[r:P:32, :, :].bitcast(I32), in_=ws_v[r].bitcast(I32))
+        nc.sync.dma_start(out=x_raw[0][:], in_=x8_v[0])
+        nc.sync.dma_start(out=x_raw[1][:], in_=x8_v[1])
+        nc.sync.dma_start(out=x4w[:], in_=x4_words.rearrange("a p n -> p a n"))
+        nc.sync.dma_start(out=w4w[:], in_=w4_words.rearrange("a p n -> p a n"))
+        nc.scalar.activation(out=junk2[:], in_=junk[:], func=SILU)
+        for piece in PIECES:
+            g = piece[0][1]
+            n0, n1 = starts[piece[0][0]], starts[piece[-1][0]] + CHUNKS[piece[-1][0]]
+            raw = sb.tile([P, PACK, n1 - n0], F32, name="w_raw%d_%d" % (piece[0][0], g))
+            for c, gg in piece:
+                w_src[(c, g)] = raw[:, :, starts[c] - n0 : starts[c] - n0 + CHUNKS[c]]
+            nc.sync.dma_start(out=raw[:], in_=w8_v[g][:, :, n0:n1])
+
+        def prep_x(g):
+            interleave(nc.vector.tensor_copy, x_grp[g], x_raw[g], 0, 320)
+            interleave(nc.scalar.copy, x_grp[g], x_raw[g], 320, T)
+            nc.vector.quantize_mx(out=x_cod[g][:].bitcast(FP8X4), scales=x_scl[g][:], in_=x_grp[g][:].rearrange("p t j -> p (t j)"))
+
+        prep_x(0)
+        for h in range(2):
+            bp = psum.tile([P, 4, P], F32, name="bp%d" % h, tag="t%d" % h)
+            for c in range(4):
+                nc.tensor.transpose(bp[:, c, :], b_col[:, 4 * h + c : 4 * h + c + 1].to_broadcast([P, P]), ident[:])
+            nc.scalar.copy(
+                out=bias[:].rearrange("q (p c) -> q p c", c=8)[:, :, 4 * h : 4 * h + 4],
+                in_=bp[:].rearrange("q c p -> q p c"),
+            )
+
+        prep_x(1)
+
+        acc = [[None] * TT for c in range(len(CHUNKS))]
+
+        def bank(c, t):
+            if acc[c][t] is None:
+                a_t = psum.tile([P, CHUNKS[c]], F32, name="acc%d_%d" % (c, t), tag="t%d" % t)
+                acc[c][t] = a_t
+            return acc[c][t]
+
+        def passes4(c, a0, a1, first):
+            n0, w = starts[c], CHUNKS[c]
+            for t in range(TT):
+                for a in range(a0, a1):
+                    nc.tensor.matmul_mx(
+                        out=bank(c, t)[:],
+                        lhsT=x4w[:, a, 2 * P * t : 2 * P * (t + 1)].bitcast(FP4X4),
+                        lhsT_scale=x4s[:, a, P * t : P * (t + 1)],
+                        rhs=w4w[:, a, 2 * n0 : 2 * (n0 + w)].bitcast(FP4X4),
+                        rhs_scale=w4s[:, a, n0 : n0 + w],
+                        start=(first and a == a0),
+                        stop=False,
+                    )
+
+        def passes8(c, g, first):
+            for t in range(TT):
+                nc.tensor.matmul_mx(
+                    out=bank(c, t)[:],
+                    lhsT=x_cod[g][:, P * t : P * (t + 1)].bitcast(FP8X4),
+                    lhsT_scale=x_scl[g][:, P * t : P * (t + 1)],
+                    rhs=w_cod[c][g][:].bitcast(FP8X4),
+                    rhs_scale=w_scl[c][g][:],
+                    start=first,
+                    stop=(g == G8 - 1),
+                )
+
+        def vcopy(c, g):
+            interleave(nc.vector.tensor_copy, w_grp[c][g], w_src[(c, g)], 0, V_COLS[c][g])
+
+        def scopy(c, g):
+            interleave(nc.scalar.copy, w_grp[c][g], w_src[(c, g)], V_COLS[c][g], CHUNKS[c])
+
+        def quant(c, g):
+            nc.vector.quantize_mx(out=w_cod[c][g][:].bitcast(FP8X4), scales=w_scl[c][g][:], in_=w_grp[c][g][:].rearrange("p n j -> p (n j)"))
+
+        def finish(c, t, parts=1):
+            n0, w = starts[c], CHUNKS[c] // parts
+            for h in range(parts):
+                z = sb.tile([P, w], F32, name="z%d_%d_%d" % (c, t, h))
+                y = sb.tile([P, w], F32, name="y%d_%d_%d" % (c, t, h))
+                cols = slice(n0 + h * w, n0 + (h + 1) * w)
+                nc.vector.tensor_add(out=z[:], in0=acc[c][t][:, h * w : (h + 1) * w], in1=bias[:, cols])
+                nc.scalar.activation(out=y[:], in_=z[:], func=SILU)
+                nc.sync.dma_start(out=out[P * t : P * (t + 1), cols], in_=y[:])
+
+        passes4(0, 0, G4, True)
+        STEPS = [
+            (vcopy, 0, 0),
+            (scopy, 0, 0),
+            (quant, 0, 0),
+            (passes8, 0, 0, False),
+            (vcopy, 0, 1),
+            (scopy, 0, 1),
+            (quant, 0, 1),
+            (passes8, 0, 1, False),
+            (passes4, 1, 0, 3, True),
+            (finish, 0, 0),
+            (finish, 0, 1),
+            (vcopy, 1, 0),
+            (scopy, 1, 0),
+            (finish, 0, 2),
+            (quant, 1, 0),
+            (passes8, 1, 0, False),
+            (vcopy, 2, 0),
+            (scopy, 2, 0),
+            (finish, 0, 3),
+            (passes4, 2, 0, 3, True),
+            (quant, 2, 0),
+            (passes8, 2, 0, False),
+            (vcopy, 1, 1),
+            (scopy, 1, 1),
+            (quant, 1, 1),
+            (passes8, 1, 1, False),
+            (vcopy, 2, 1),
+            (scopy, 2, 1),
+            (finish, 1, 0),
+            (quant, 2, 1),
+            (passes8, 2, 1, False),
+            (finish, 1, 1),
+            (finish, 1, 2),
+            (finish, 1, 3),
+            (finish, 2, 0),
+            (finish, 2, 1),
+            (finish, 2, 2),
+            (finish, 2, 3),
+        ]
+        for step in STEPS:
+            step[0](*step[1:])

@@ -19,13 +19,11 @@ T, N = 512, 1024
 K8, K4 = 1024, 1536
 G8, G4 = K8 // K_PASS, K4 // K_PASS
 TT = T // P
+BANK = 512
+HALF = N // 2
+QUARTER = N // 4
 
 FLOPS = 2 * (K8 + K4) * T * N
-
-CHUNKS = [256,512,256]
-V_COLS = [[160,160],[320,320],[160,160]]
-PIECES = [[(0, 0)], [(0, 1)], [(1, 0), (2, 0)], [(1, 1)], [(2, 1)]]
-STORE_GROUPS = [[0],[1],[2]]
 
 
 def interleave(copy, grouped, raw, c0, c1):
@@ -39,19 +37,9 @@ def tile_mix_atom_tm_silu_kernel(tc, x8, w8, x4_words, x4_scales, w4_words, w4_s
     nc = tc.nc
     with ExitStack() as ctx:
         sb = ctx.enter_context(tc.tile_pool(name="sb", bufs=1))
-        psum = ctx.enter_context(tc.psum_pool(name="psum", bufs=2))
+        psum = ctx.enter_context(tc.psum_pool(name="psum", bufs=1))
         ctx.enter_context(tc.manual_schedule())
 
-        starts = [sum(CHUNKS[:c]) for c in range(len(CHUNKS))]
-
-        x_raw = [sb.tile([P, PACK, T], F32, name="x_raw%d" % g) for g in range(G8)]
-        x_grp = [sb.tile([P, T, PACK], BF16, name="x_grp%d" % g, align_bytes=64) for g in range(G8)]
-        x_cod = [sb.tile([P, T], U32, name="x_cod%d" % g, align_bytes=64) for g in range(G8)]
-        x_scl = [sb.tile([P, T], U8, name="x_scl%d" % g, align_bytes=64) for g in range(G8)]
-        w_src = {}
-        w_grp = [[sb.tile([P, CHUNKS[c], PACK], BF16, name="w_grp%d_%d" % (c, g), align_bytes=64) for g in range(G8)] for c in range(len(CHUNKS))]
-        w_cod = [[sb.tile([P, CHUNKS[c]], U32, name="w_cod%d_%d" % (c, g), align_bytes=64) for g in range(G8)] for c in range(len(CHUNKS))]
-        w_scl = [[sb.tile([P, CHUNKS[c]], U8, name="w_scl%d_%d" % (c, g), align_bytes=64) for g in range(G8)] for c in range(len(CHUNKS))]
         x4w = sb.tile([P, G4, 2 * T], U8, name="x4w", align_bytes=64)
         w4w = sb.tile([P, G4, 2 * N], U8, name="w4w", align_bytes=64)
         x4s = sb.tile([P, G4, T], U8, name="x4s", align_bytes=64)
@@ -59,149 +47,165 @@ def tile_mix_atom_tm_silu_kernel(tc, x8, w8, x4_words, x4_scales, w4_words, w4_s
         b_col = sb.tile([P, N // P], F32, name="b_col")
         ident = sb.tile([P, P], F32, name="ident")
         bias = sb.tile([P, N], F32, name="bias")
-        junk = sb.tile([P, 1], F32, name="junk")
-        junk2 = sb.tile([P, 1], F32, name="junk2")
-
-        nc.vector.memset(x4s[:].rearrange("p a n -> p (a n)").bitcast(I32), 0)
-        nc.vector.memset(junk[:], 0.0)
-        nc.vector.memset(w4s[:].rearrange("p a n -> p (a n)").bitcast(I32), 0)
+        warm_in = sb.tile([P, 1], F32, name="warm_in")
+        warm_out = sb.tile([P, 1], F32, name="warm_out")
 
         x8_v = x8.rearrange("(g p j) t -> g p j t", p=P, j=PACK)
         w8_v = w8.rearrange("(g p j) n -> g p j n", p=P, j=PACK)
         ws_v = w4_scales.rearrange("a (q r) n -> r q a n", r=4)
         xs_v = x4_scales.rearrange("a (q r) n -> r q a n", r=4)
 
+        sources = {
+            "x0": x8_v[0],
+            "w0a": w8_v[0][:, :, 0:HALF],
+            "x1": x8_v[1],
+            "w1a": w8_v[1][:, :, 0:HALF],
+            "w0b": w8_v[0][:, :, HALF:N],
+            "w1c": w8_v[1][:, :, HALF : HALF + QUARTER],
+            "w1d": w8_v[1][:, :, HALF + QUARTER : N],
+        }
+        raw, grouped, codes, scales = {}, {}, {}, {}
+        for key, src in sources.items():
+            width = src.shape[2]
+            raw[key] = sb.tile([P, PACK, width], F32, name="raw_" + key)
+            grouped[key] = sb.tile([P, width, PACK], BF16, name="grouped_" + key, align_bytes=64)
+            codes[key] = sb.tile([P, width], U32, name="codes_" + key, align_bytes=64)
+            scales[key] = sb.tile([P, width], U8, name="scales_" + key, align_bytes=64)
+
+        nc.vector.memset(x4s[:].rearrange("p a n -> p (a n)").bitcast(I32), 0)
+        nc.vector.memset(w4s[:].rearrange("p a n -> p (a n)").bitcast(I32), 0)
+        nc.vector.memset(warm_in[:], 0.0)
+
         nc.gpsimd.dma_start(out=b_col[:], in_=b.rearrange("(p c) -> p c", p=P))
         make_identity(nc, ident[:])
-        for r in range(4):
-            nc.scalar.dma_start(out=x4s[r:P:32, :, :].bitcast(I32), in_=xs_v[r].bitcast(I32))
-        for r in range(2):
-            nc.scalar.dma_start(out=w4s[r:P:32, :, :].bitcast(I32), in_=ws_v[r].bitcast(I32))
-        for r in range(2, 4):
-            nc.gpsimd.dma_start(out=w4s[r:P:32, :, :].bitcast(I32), in_=ws_v[r].bitcast(I32))
-        nc.sync.dma_start(out=x_raw[0][:], in_=x8_v[0])
-        nc.sync.dma_start(out=x_raw[1][:], in_=x8_v[1])
-        nc.sync.dma_start(out=x4w[:], in_=x4_words.rearrange("a p n -> p a n"))
         nc.sync.dma_start(out=w4w[:], in_=w4_words.rearrange("a p n -> p a n"))
-        nc.scalar.activation(out=junk2[:], in_=junk[:], func=SILU)
-        for piece in PIECES:
-            g = piece[0][1]
-            n0, n1 = starts[piece[0][0]], starts[piece[-1][0]] + CHUNKS[piece[-1][0]]
-            raw = sb.tile([P, PACK, n1 - n0], F32, name="w_raw%d_%d" % (piece[0][0], g))
-            for c, gg in piece:
-                w_src[(c, g)] = raw[:, :, starts[c] - n0 : starts[c] - n0 + CHUNKS[c]]
-            nc.sync.dma_start(out=raw[:], in_=w8_v[g][:, :, n0:n1])
+        for r in range(4):
+            nc.sync.dma_start(out=x4s[r:P:32, :, :].bitcast(I32), in_=xs_v[r].bitcast(I32))
+        nc.sync.dma_start(out=x4w[:], in_=x4_words.rearrange("a p n -> p a n"))
+        for r in range(4):
+            nc.sync.dma_start(out=w4s[r:P:32, :, :].bitcast(I32), in_=ws_v[r].bitcast(I32))
+        for key, src in sources.items():
+            nc.sync.dma_start(out=raw[key][:], in_=src)
+        nc.scalar.activation(out=warm_out[:], in_=warm_in[:], func=SILU)
 
-        def prep_x(g):
-            interleave(nc.vector.tensor_copy, x_grp[g], x_raw[g], 0, 320)
-            interleave(nc.scalar.copy, x_grp[g], x_raw[g], 320, T)
-            nc.vector.quantize_mx(out=x_cod[g][:].bitcast(FP8X4), scales=x_scl[g][:], in_=x_grp[g][:].rearrange("p t j -> p (t j)"))
-
-        prep_x(0)
-        for h in range(2):
-            bp = psum.tile([P, 4, P], F32, name="bp%d" % h, tag="t%d" % h)
+        for h, copy in enumerate([nc.vector.tensor_copy, nc.scalar.copy]):
+            bp = psum.tile([P, 4, P], F32, name="bp%d" % h, tag="bank%d" % (6 + h))
             for c in range(4):
                 nc.tensor.transpose(bp[:, c, :], b_col[:, 4 * h + c : 4 * h + c + 1].to_broadcast([P, P]), ident[:])
-            nc.scalar.copy(
+            copy(
                 out=bias[:].rearrange("q (p c) -> q p c", c=8)[:, :, 4 * h : 4 * h + 4],
                 in_=bp[:].rearrange("q c p -> q p c"),
             )
 
-        prep_x(1)
+        layout = [([t], 0, HALF) for t in range(TT)]
+        layout = layout + [([t, t + 1], n0, QUARTER) for n0 in (HALF, HALF + QUARTER) for t in (0, 2)]
+        acc = []
+        for i, (tiles, n0, width) in enumerate(layout):
+            bank_tile = psum.tile([P, len(tiles), width], F32, name="acc%d" % i, tag="bank%d" % i)
+            acc.append(bank_tile)
+        opened = set()
 
-        acc = [[None] * TT for c in range(len(CHUNKS))]
-
-        def bank(c, t):
-            if acc[c][t] is None:
-                a_t = psum.tile([P, CHUNKS[c]], F32, name="acc%d_%d" % (c, t), tag="t%d" % t)
-                acc[c][t] = a_t
-            return acc[c][t]
-
-        def passes4(c, a0, a1, first):
-            n0, w = starts[c], CHUNKS[c]
-            for t in range(TT):
-                for a in range(a0, a1):
+        def fp4(i):
+            tiles, n0, width = layout[i]
+            for s, t in enumerate(tiles):
+                for a in range(G4):
                     nc.tensor.matmul_mx(
-                        out=bank(c, t)[:],
+                        out=acc[i][:, s, :],
                         lhsT=x4w[:, a, 2 * P * t : 2 * P * (t + 1)].bitcast(FP4X4),
                         lhsT_scale=x4s[:, a, P * t : P * (t + 1)],
-                        rhs=w4w[:, a, 2 * n0 : 2 * (n0 + w)].bitcast(FP4X4),
-                        rhs_scale=w4s[:, a, n0 : n0 + w],
-                        start=(first and a == a0),
+                        rhs=w4w[:, a, 2 * n0 : 2 * (n0 + width)].bitcast(FP4X4),
+                        rhs_scale=w4s[:, a, n0 : n0 + width],
+                        start=i not in opened,
                         stop=False,
                     )
+                    opened.add(i)
 
-        def passes8(c, g, first):
-            for t in range(TT):
+        def fp8(i, xkey, wkey, c0, last):
+            tiles, n0, width = layout[i]
+            for s, t in enumerate(tiles):
                 nc.tensor.matmul_mx(
-                    out=bank(c, t)[:],
-                    lhsT=x_cod[g][:, P * t : P * (t + 1)].bitcast(FP8X4),
-                    lhsT_scale=x_scl[g][:, P * t : P * (t + 1)],
-                    rhs=w_cod[c][g][:].bitcast(FP8X4),
-                    rhs_scale=w_scl[c][g][:],
-                    start=first,
-                    stop=(g == G8 - 1),
+                    out=acc[i][:, s, :],
+                    lhsT=codes[xkey][:, P * t : P * (t + 1)].bitcast(FP8X4),
+                    lhsT_scale=scales[xkey][:, P * t : P * (t + 1)],
+                    rhs=codes[wkey][:, c0 : c0 + width].bitcast(FP8X4),
+                    rhs_scale=scales[wkey][:, c0 : c0 + width],
+                    start=i not in opened,
+                    stop=last and s == len(tiles) - 1,
                 )
+                opened.add(i)
 
-        def vcopy(c, g):
-            interleave(nc.vector.tensor_copy, w_grp[c][g], w_src[(c, g)], 0, V_COLS[c][g])
+        def vcopy(key, share=8):
+            interleave(nc.vector.tensor_copy, grouped[key], raw[key], 0, sources[key].shape[2] * share // 16)
 
-        def scopy(c, g):
-            interleave(nc.scalar.copy, w_grp[c][g], w_src[(c, g)], V_COLS[c][g], CHUNKS[c])
+        def scopy(key, share=8):
+            interleave(nc.scalar.copy, grouped[key], raw[key], sources[key].shape[2] * share // 16, sources[key].shape[2])
 
-        def quant(c, g):
-            nc.vector.quantize_mx(out=w_cod[c][g][:].bitcast(FP8X4), scales=w_scl[c][g][:], in_=w_grp[c][g][:].rearrange("p n j -> p (n j)"))
+        def quant(key):
+            nc.vector.quantize_mx(
+                out=codes[key][:].bitcast(FP8X4),
+                scales=scales[key][:],
+                in_=grouped[key][:].rearrange("p n j -> p (n j)"),
+            )
 
-        def finish(c, t, parts=1):
-            n0, w = starts[c], CHUNKS[c] // parts
-            for h in range(parts):
-                z = sb.tile([P, w], F32, name="z%d_%d_%d" % (c, t, h))
-                y = sb.tile([P, w], F32, name="y%d_%d_%d" % (c, t, h))
-                cols = slice(n0 + h * w, n0 + (h + 1) * w)
-                nc.vector.tensor_add(out=z[:], in0=acc[c][t][:, h * w : (h + 1) * w], in1=bias[:, cols])
-                nc.scalar.activation(out=y[:], in_=z[:], func=SILU)
-                nc.sync.dma_start(out=out[P * t : P * (t + 1), cols], in_=y[:])
+        def prep(key, share=10):
+            vcopy(key, share)
+            scopy(key, share)
+            quant(key)
 
-        passes4(0, 0, G4, True)
-        STEPS = [
-            (vcopy, 0, 0),
-            (scopy, 0, 0),
-            (quant, 0, 0),
-            (passes8, 0, 0, False),
-            (vcopy, 0, 1),
-            (scopy, 0, 1),
-            (quant, 0, 1),
-            (passes8, 0, 1, False),
-            (passes4, 1, 0, 3, True),
-            (finish, 0, 0),
-            (finish, 0, 1),
-            (vcopy, 1, 0),
-            (scopy, 1, 0),
-            (finish, 0, 2),
-            (quant, 1, 0),
-            (passes8, 1, 0, False),
-            (vcopy, 2, 0),
-            (scopy, 2, 0),
-            (finish, 0, 3),
-            (passes4, 2, 0, 3, True),
-            (quant, 2, 0),
-            (passes8, 2, 0, False),
-            (vcopy, 1, 1),
-            (scopy, 1, 1),
-            (quant, 1, 1),
-            (passes8, 1, 1, False),
-            (vcopy, 2, 1),
-            (scopy, 2, 1),
-            (finish, 1, 0),
-            (quant, 2, 1),
-            (passes8, 2, 1, False),
-            (finish, 1, 1),
-            (finish, 1, 2),
-            (finish, 1, 3),
-            (finish, 2, 0),
-            (finish, 2, 1),
-            (finish, 2, 2),
-            (finish, 2, 3),
-        ]
-        for step in STEPS:
-            step[0](*step[1:])
+        summed = {}
+
+        def add(i):
+            tiles, n0, width = layout[i]
+            z = sb.tile([P, len(tiles), width], F32, name="z%d" % i)
+            summed[i] = z
+            row = bias[:, n0 : n0 + width].rearrange("p (o n) -> p o n", o=1)
+            nc.vector.tensor_add(out=z[:], in0=acc[i][:], in1=row.to_broadcast([P, len(tiles), width]))
+
+        def silu_store(i):
+            tiles, n0, width = layout[i]
+            y = sb.tile([P, len(tiles), width], F32, name="y%d" % i)
+            nc.scalar.activation(out=y[:], in_=summed[i][:], func=SILU)
+            rows = out[P * tiles[0] : P * (tiles[-1] + 1), n0 : n0 + width]
+            nc.sync.dma_start(out=rows.rearrange("(s p) n -> p s n", p=P), in_=y[:])
+
+        for i in range(4):
+            fp4(i)
+        prep("x0")
+        prep("w0a")
+        for i in range(4):
+            fp8(i, "x0", "w0a", 0, False)
+        for i in range(4, 7):
+            fp4(i)
+        prep("x1")
+        prep("w1a")
+        for i in range(4):
+            fp8(i, "x1", "w1a", 0, True)
+        fp4(7)
+        add(0)
+        vcopy("w0b")
+        scopy("w0b")
+        silu_store(0)
+        add(1)
+        quant("w0b")
+        for i in range(4, 8):
+            fp8(i, "x0", "w0b", layout[i][1] - HALF, False)
+        vcopy("w1c")
+        scopy("w1c")
+        silu_store(1)
+        add(2)
+        quant("w1c")
+        fp8(4, "x1", "w1c", 0, True)
+        fp8(5, "x1", "w1c", 0, True)
+        silu_store(2)
+        add(3)
+        vcopy("w1d")
+        scopy("w1d")
+        silu_store(3)
+        add(4)
+        quant("w1d")
+        fp8(6, "x1", "w1d", 0, True)
+        fp8(7, "x1", "w1d", 0, True)
+        silu_store(4)
+        for i in range(5, 8):
+            add(i)
+            silu_store(i)

@@ -58,8 +58,8 @@ def tile_mix_atom_tm_silu_kernel(tc, x8, w8, x4_words, x4_scales, w4_words, w4_s
         sources = {
             "x0": x8_v[0],
             "w0a": w8_v[0][:, :, 0:HALF],
-            "x1": x8_v[1],
             "w1a": w8_v[1][:, :, 0:HALF],
+            "x1": x8_v[1],
             "w0b": w8_v[0][:, :, HALF:N],
             "w1c": w8_v[1][:, :, HALF : HALF + QUARTER],
             "w1d": w8_v[1][:, :, HALF + QUARTER : N],
@@ -134,22 +134,22 @@ def tile_mix_atom_tm_silu_kernel(tc, x8, w8, x4_words, x4_scales, w4_words, w4_s
                 )
                 opened.add(i)
 
-        def vcopy(key, share=8):
-            interleave(nc.vector.tensor_copy, grouped[key], raw[key], 0, sources[key].shape[2] * share // 16)
+        def vcopy(key, c0, c1):
+            interleave(nc.vector.tensor_copy, grouped[key], raw[key], c0, c1)
 
-        def scopy(key, share=8):
-            interleave(nc.scalar.copy, grouped[key], raw[key], sources[key].shape[2] * share // 16, sources[key].shape[2])
+        def scopy(key, c0, c1):
+            interleave(nc.scalar.copy, grouped[key], raw[key], c0, c1)
 
-        def quant(key):
+        def quant(key, c0=0, c1=None):
             nc.vector.quantize_mx(
-                out=codes[key][:].bitcast(FP8X4),
-                scales=scales[key][:],
-                in_=grouped[key][:].rearrange("p n j -> p (n j)"),
+                out=codes[key][:, c0:c1].bitcast(FP8X4),
+                scales=scales[key][:, c0:c1],
+                in_=grouped[key][:, c0:c1, :].rearrange("p n j -> p (n j)"),
             )
 
-        def prep(key, share=10):
-            vcopy(key, share)
-            scopy(key, share)
+        def prep(key):
+            vcopy(key, 0, 320)
+            scopy(key, 320, HALF)
             quant(key)
 
         summed = {}
@@ -168,44 +168,63 @@ def tile_mix_atom_tm_silu_kernel(tc, x8, w8, x4_words, x4_scales, w4_words, w4_s
             rows = out[P * tiles[0] : P * (tiles[-1] + 1), n0 : n0 + width]
             nc.sync.dma_start(out=rows.rearrange("(s p) n -> p s n", p=P), in_=y[:])
 
+        def finish_tile(i, s, queue):
+            tiles, n0, width = layout[i]
+            t = tiles[s]
+            z = sb.tile([P, width], F32, name="z_tile%d_%d" % (i, s))
+            y = sb.tile([P, width], F32, name="y_tile%d_%d" % (i, s))
+            nc.vector.tensor_add(out=z[:], in0=acc[i][:, s, :], in1=bias[:, n0 : n0 + width])
+            nc.scalar.activation(out=y[:], in_=z[:], func=SILU)
+            queue.dma_start(out=out[P * t : P * (t + 1), n0 : n0 + width], in_=y[:])
+
         for i in range(4):
             fp4(i)
         prep("x0")
         prep("w0a")
+        fp4(4)
         for i in range(4):
             fp8(i, "x0", "w0a", 0, False)
-        for i in range(4, 7):
+        for i in range(5, 7):
             fp4(i)
-        prep("x1")
         prep("w1a")
-        for i in range(4):
-            fp8(i, "x1", "w1a", 0, True)
+        vcopy("x1", 0, P)
+        scopy("x1", 2 * P, 3 * P)
+        vcopy("x1", P, 2 * P)
+        scopy("x1", 3 * P, 4 * P)
+        for t in range(TT):
+            quant("x1", P * t, P * (t + 1))
+            fp8(t, "x1", "w1a", 0, True)
         fp4(7)
         add(0)
-        vcopy("w0b")
-        scopy("w0b")
-        silu_store(0)
+        vcopy("w0b", 0, 256)
+        scopy("w0b", 256, 512)
         add(1)
-        quant("w0b")
-        for i in range(4, 8):
+        quant("w0b", 0, 256)
+        silu_store(0)
+        for i in range(4, 6):
             fp8(i, "x0", "w0b", layout[i][1] - HALF, False)
-        vcopy("w1c")
-        scopy("w1c")
+        quant("w0b", 256, 512)
+        vcopy("w1c", 0, 128)
+        scopy("w1c", 128, 256)
         silu_store(1)
         add(2)
         quant("w1c")
         fp8(4, "x1", "w1c", 0, True)
         fp8(5, "x1", "w1c", 0, True)
+        for i in range(6, 8):
+            fp8(i, "x0", "w0b", layout[i][1] - HALF, False)
         silu_store(2)
         add(3)
-        vcopy("w1d")
-        scopy("w1d")
+        vcopy("w1d", 0, 128)
+        scopy("w1d", 128, 256)
         silu_store(3)
         add(4)
         quant("w1d")
         fp8(6, "x1", "w1d", 0, True)
         fp8(7, "x1", "w1d", 0, True)
         silu_store(4)
-        for i in range(5, 8):
-            add(i)
-            silu_store(i)
+        add(5)
+        silu_store(5)
+        for i in (6, 7):
+            finish_tile(i, 0, nc.sync)
+            finish_tile(i, 1, nc.sync)

@@ -78,10 +78,10 @@ def tile_mix_atom_tm_silu_kernel(tc, x8, w8, x4_words, x4_scales, w4_words, w4_s
 
         nc.gpsimd.dma_start(out=b_col[:], in_=b.rearrange("(p c) -> p c", p=P))
         make_identity(nc, ident[:])
-        nc.sync.dma_start(out=w4w[:], in_=w4_words.rearrange("a p n -> p a n"))
+        nc.sync.dma_start(out=x4w[:], in_=x4_words.rearrange("a p n -> p a n"))
         for r in range(4):
             nc.sync.dma_start(out=x4s[r:P:32, :, :].bitcast(I32), in_=xs_v[r].bitcast(I32))
-        nc.sync.dma_start(out=x4w[:], in_=x4_words.rearrange("a p n -> p a n"))
+        nc.sync.dma_start(out=w4w[:], in_=w4_words.rearrange("a p n -> p a n"))
         for r in range(4):
             nc.sync.dma_start(out=w4s[r:P:32, :, :].bitcast(I32), in_=ws_v[r].bitcast(I32))
         for key, src in sources.items():
@@ -148,9 +148,10 @@ def tile_mix_atom_tm_silu_kernel(tc, x8, w8, x4_words, x4_scales, w4_words, w4_s
             )
 
         def prep(key):
-            vcopy(key, 0, 320)
-            scopy(key, 320, HALF)
-            quant(key)
+            vcopy(key, 0, QUARTER)
+            scopy(key, QUARTER, HALF)
+            quant(key, 0, QUARTER)
+            quant(key, QUARTER, HALF)
 
         summed = {}
 
@@ -187,15 +188,18 @@ def tile_mix_atom_tm_silu_kernel(tc, x8, w8, x4_words, x4_scales, w4_words, w4_s
         for i in range(5, 7):
             fp4(i)
         prep("w1a")
-        vcopy("x1", 0, P)
-        scopy("x1", 2 * P, 3 * P)
+        vcopy("x1", 0, P // 2)
+        scopy("x1", P // 2, P)
         vcopy("x1", P, 2 * P)
+        scopy("x1", 2 * P, 3 * P)
         scopy("x1", 3 * P, 4 * P)
-        for t in range(TT):
+        for t in range(TT - 1):
             quant("x1", P * t, P * (t + 1))
             fp8(t, "x1", "w1a", 0, True)
-        fp4(7)
         add(0)
+        quant("x1", 3 * P, 4 * P)
+        fp8(3, "x1", "w1a", 0, True)
+        fp4(7)
         vcopy("w0b", 0, 256)
         scopy("w0b", 256, 512)
         add(1)
@@ -223,8 +227,6 @@ def tile_mix_atom_tm_silu_kernel(tc, x8, w8, x4_words, x4_scales, w4_words, w4_s
         fp8(6, "x1", "w1d", 0, True)
         fp8(7, "x1", "w1d", 0, True)
         silu_store(4)
-        add(5)
-        silu_store(5)
-        for i in (6, 7):
+        for i in range(5, 8):
             finish_tile(i, 0, nc.sync)
             finish_tile(i, 1, nc.sync)

@@ -41,7 +41,8 @@ def tile_mix_atom_tm_silu_kernel(tc, x8, w8, x4_words, x4_scales, w4_words, w4_s
         ctx.enter_context(tc.manual_schedule())
 
         x4w = sb.tile([P, G4, 2 * T], U8, name="x4w", align_bytes=64)
-        w4w = sb.tile([P, G4, 2 * N], U8, name="w4w", align_bytes=64)
+        w4w_left = sb.tile([P, G4, 2 * HALF], U8, name="w4w_left", align_bytes=64)
+        w4w_right = sb.tile([P, G4, 2 * HALF], U8, name="w4w_right", align_bytes=64)
         x4s = sb.tile([P, G4, T], U8, name="x4s", align_bytes=64)
         w4s = sb.tile([P, G4, N], U8, name="w4s", align_bytes=64)
         b_col = sb.tile([P, N // P], F32, name="b_col")
@@ -52,6 +53,7 @@ def tile_mix_atom_tm_silu_kernel(tc, x8, w8, x4_words, x4_scales, w4_words, w4_s
 
         x8_v = x8.rearrange("(g p j) t -> g p j t", p=P, j=PACK)
         w8_v = w8.rearrange("(g p j) n -> g p j n", p=P, j=PACK)
+        w4_v = w4_words.rearrange("a p n -> p a n")
         ws_v = w4_scales.rearrange("a (q r) n -> r q a n", r=4)
         xs_v = x4_scales.rearrange("a (q r) n -> r q a n", r=4)
 
@@ -81,39 +83,53 @@ def tile_mix_atom_tm_silu_kernel(tc, x8, w8, x4_words, x4_scales, w4_words, w4_s
         nc.sync.dma_start(out=x4w[:], in_=x4_words.rearrange("a p n -> p a n"))
         for r in range(4):
             nc.sync.dma_start(out=x4s[r:P:32, :, :].bitcast(I32), in_=xs_v[r].bitcast(I32))
-        nc.sync.dma_start(out=w4w[:], in_=w4_words.rearrange("a p n -> p a n"))
+        nc.sync.dma_start(out=raw["x0"][:], in_=sources["x0"])
+        nc.sync.dma_start(out=w4w_left[:], in_=w4_v[:, :, 0 : 2 * HALF])
         for r in range(4):
             nc.sync.dma_start(out=w4s[r:P:32, :, :].bitcast(I32), in_=ws_v[r].bitcast(I32))
         for key, src in sources.items():
-            nc.sync.dma_start(out=raw[key][:], in_=src)
+            if key != "x0":
+                nc.sync.dma_start(out=raw[key][:], in_=src)
+            if key == "x1":
+                nc.sync.dma_start(out=w4w_right[:], in_=w4_v[:, :, 2 * HALF : 2 * N])
         nc.scalar.activation(out=warm_out[:], in_=warm_in[:], func=SILU)
 
-        for h, copy in enumerate([nc.vector.tensor_copy, nc.scalar.copy]):
+        spread = []
+        for h in range(2):
             bp = psum.tile([P, 4, P], F32, name="bp%d" % h, tag="bank%d" % (6 + h))
+            spread.append(bp)
             for c in range(4):
                 nc.tensor.transpose(bp[:, c, :], b_col[:, 4 * h + c : 4 * h + c + 1].to_broadcast([P, P]), ident[:])
-            copy(
-                out=bias[:].rearrange("q (p c) -> q p c", c=8)[:, :, 4 * h : 4 * h + 4],
-                in_=bp[:].rearrange("q c p -> q p c"),
-            )
+
+        def copy_bias():
+            for h, copy in enumerate([nc.vector.tensor_copy, nc.scalar.copy]):
+                copy(
+                    out=bias[:].rearrange("q (p c) -> q p c", c=8)[:, :, 4 * h : 4 * h + 4],
+                    in_=spread[h][:].rearrange("q c p -> q p c"),
+                )
 
         layout = [([t], 0, HALF) for t in range(TT)]
         layout = layout + [([t, t + 1], n0, QUARTER) for n0 in (HALF, HALF + QUARTER) for t in (0, 2)]
         acc = []
-        for i, (tiles, n0, width) in enumerate(layout):
-            bank_tile = psum.tile([P, len(tiles), width], F32, name="acc%d" % i, tag="bank%d" % i)
-            acc.append(bank_tile)
+
+        def open_banks(first, last):
+            for i in range(first, last):
+                tiles, n0, width = layout[i]
+                bank_tile = psum.tile([P, len(tiles), width], F32, name="acc%d" % i, tag="bank%d" % i)
+                acc.append(bank_tile)
+
         opened = set()
 
         def fp4(i):
             tiles, n0, width = layout[i]
+            words, c0 = (w4w_left, n0) if n0 < HALF else (w4w_right, n0 - HALF)
             for s, t in enumerate(tiles):
                 for a in range(G4):
                     nc.tensor.matmul_mx(
                         out=acc[i][:, s, :],
                         lhsT=x4w[:, a, 2 * P * t : 2 * P * (t + 1)].bitcast(FP4X4),
                         lhsT_scale=x4s[:, a, P * t : P * (t + 1)],
-                        rhs=w4w[:, a, 2 * n0 : 2 * (n0 + width)].bitcast(FP4X4),
+                        rhs=words[:, a, 2 * c0 : 2 * (c0 + width)].bitcast(FP4X4),
                         rhs_scale=w4s[:, a, n0 : n0 + width],
                         start=i not in opened,
                         stop=False,
@@ -169,6 +185,19 @@ def tile_mix_atom_tm_silu_kernel(tc, x8, w8, x4_words, x4_scales, w4_words, w4_s
             rows = out[P * tiles[0] : P * (tiles[-1] + 1), n0 : n0 + width]
             nc.sync.dma_start(out=rows.rearrange("(s p) n -> p s n", p=P), in_=y[:])
 
+        def add_tile(i, s):
+            tiles, n0, width = layout[i]
+            z = sb.tile([P, width], F32, name="z_tile%d_%d" % (i, s))
+            summed[(i, s)] = z
+            nc.vector.tensor_add(out=z[:], in0=acc[i][:, s, :], in1=bias[:, n0 : n0 + width])
+
+        def silu_tile(i, s):
+            tiles, n0, width = layout[i]
+            t = tiles[s]
+            y = sb.tile([P, width], F32, name="y_tile%d_%d" % (i, s))
+            nc.scalar.activation(out=y[:], in_=summed[(i, s)][:], func=SILU)
+            nc.sync.dma_start(out=out[P * t : P * (t + 1), n0 : n0 + width], in_=y[:])
+
         def finish_tile(i, s, queue):
             tiles, n0, width = layout[i]
             t = tiles[s]
@@ -178,55 +207,59 @@ def tile_mix_atom_tm_silu_kernel(tc, x8, w8, x4_words, x4_scales, w4_words, w4_s
             nc.scalar.activation(out=y[:], in_=z[:], func=SILU)
             queue.dma_start(out=out[P * t : P * (t + 1), n0 : n0 + width], in_=y[:])
 
-        for i in range(4):
+        open_banks(0, 6)
+        for i in range(3):
             fp4(i)
         prep("x0")
+        copy_bias()
+        open_banks(6, 8)
         prep("w0a")
-        fp4(4)
         for i in range(4):
             fp8(i, "x0", "w0a", 0, False)
-        for i in range(5, 7):
+        for i in range(3, 4):
             fp4(i)
         prep("w1a")
         vcopy("x1", 0, P // 2)
         scopy("x1", P // 2, P)
         vcopy("x1", P, 2 * P)
         scopy("x1", 2 * P, 3 * P)
-        scopy("x1", 3 * P, 4 * P)
-        for t in range(TT - 1):
+        quant("x1", 0, P)
+        vcopy("x1", 3 * P, 4 * P)
+        for t in range(1, TT):
             quant("x1", P * t, P * (t + 1))
+        for t in range(TT):
             fp8(t, "x1", "w1a", 0, True)
-        add(0)
-        quant("x1", 3 * P, 4 * P)
-        fp8(3, "x1", "w1a", 0, True)
-        fp4(7)
+        for i in range(4, 8):
+            fp4(i)
+        for i in range(2):
+            add(i)
+            silu_store(i)
+        add(2)
         vcopy("w0b", 0, 256)
         scopy("w0b", 256, 512)
-        add(1)
+        add(3)
         quant("w0b", 0, 256)
-        silu_store(0)
         for i in range(4, 6):
             fp8(i, "x0", "w0b", layout[i][1] - HALF, False)
-        quant("w0b", 256, 512)
         vcopy("w1c", 0, 128)
         scopy("w1c", 128, 256)
-        silu_store(1)
-        add(2)
+        silu_store(2)
+        quant("w0b", 256, 512)
         quant("w1c")
         fp8(4, "x1", "w1c", 0, True)
         fp8(5, "x1", "w1c", 0, True)
         for i in range(6, 8):
             fp8(i, "x0", "w0b", layout[i][1] - HALF, False)
-        silu_store(2)
-        add(3)
         vcopy("w1d", 0, 128)
         scopy("w1d", 128, 256)
         silu_store(3)
-        add(4)
+        add_tile(4, 0)
+        add_tile(4, 1)
         quant("w1d")
         fp8(6, "x1", "w1d", 0, True)
         fp8(7, "x1", "w1d", 0, True)
-        silu_store(4)
+        silu_tile(4, 0)
+        silu_tile(4, 1)
         for i in range(5, 8):
             finish_tile(i, 0, nc.sync)
             finish_tile(i, 1, nc.sync)

@@ -40,9 +40,10 @@ def tile_mix_atom_tm_silu_kernel(tc, x8, w8, x4_words, x4_scales, w4_words, w4_s
         psum = ctx.enter_context(tc.psum_pool(name="psum", bufs=1))
         ctx.enter_context(tc.manual_schedule())
 
-        x4w = sb.tile([P, G4, 2 * T], U8, name="x4w", align_bytes=64)
-        w4w_left = sb.tile([P, G4, 2 * HALF], U8, name="w4w_left", align_bytes=64)
-        w4w_right = sb.tile([P, G4, 2 * HALF], U8, name="w4w_right", align_bytes=64)
+        x4w = sb.tile([P, G4 - 1, 2 * T], U8, name="x4w", align_bytes=64)
+        w4w = sb.tile([P, G4 - 1, 2 * N], U8, name="w4w", align_bytes=64)
+        x4w_last = sb.tile([P, 2 * T], U8, name="x4w_last", align_bytes=64)
+        w4w_last = sb.tile([P, 2 * N], U8, name="w4w_last", align_bytes=64)
         x4s = sb.tile([P, G4, T], U8, name="x4s", align_bytes=64)
         w4s = sb.tile([P, G4, N], U8, name="w4s", align_bytes=64)
         b_col = sb.tile([P, N // P], F32, name="b_col")
@@ -53,7 +54,6 @@ def tile_mix_atom_tm_silu_kernel(tc, x8, w8, x4_words, x4_scales, w4_words, w4_s
 
         x8_v = x8.rearrange("(g p j) t -> g p j t", p=P, j=PACK)
         w8_v = w8.rearrange("(g p j) n -> g p j n", p=P, j=PACK)
-        w4_v = w4_words.rearrange("a p n -> p a n")
         ws_v = w4_scales.rearrange("a (q r) n -> r q a n", r=4)
         xs_v = x4_scales.rearrange("a (q r) n -> r q a n", r=4)
 
@@ -80,18 +80,19 @@ def tile_mix_atom_tm_silu_kernel(tc, x8, w8, x4_words, x4_scales, w4_words, w4_s
 
         nc.gpsimd.dma_start(out=b_col[:], in_=b.rearrange("(p c) -> p c", p=P))
         make_identity(nc, ident[:])
-        nc.sync.dma_start(out=x4w[:], in_=x4_words.rearrange("a p n -> p a n"))
+        nc.sync.dma_start(out=x4w[:], in_=x4_words[0 : G4 - 1].rearrange("a p n -> p a n"))
         for r in range(4):
             nc.sync.dma_start(out=x4s[r:P:32, :, :].bitcast(I32), in_=xs_v[r].bitcast(I32))
         nc.sync.dma_start(out=raw["x0"][:], in_=sources["x0"])
-        nc.sync.dma_start(out=w4w_left[:], in_=w4_v[:, :, 0 : 2 * HALF])
+        nc.sync.dma_start(out=w4w[:], in_=w4_words[0 : G4 - 1].rearrange("a p n -> p a n"))
         for r in range(4):
             nc.sync.dma_start(out=w4s[r:P:32, :, :].bitcast(I32), in_=ws_v[r].bitcast(I32))
         for key, src in sources.items():
             if key != "x0":
                 nc.sync.dma_start(out=raw[key][:], in_=src)
             if key == "x1":
-                nc.sync.dma_start(out=w4w_right[:], in_=w4_v[:, :, 2 * HALF : 2 * N])
+                nc.sync.dma_start(out=x4w_last[:], in_=x4_words[G4 - 1])
+                nc.sync.dma_start(out=w4w_last[:], in_=w4_words[G4 - 1])
         nc.scalar.activation(out=warm_out[:], in_=warm_in[:], func=SILU)
 
         spread = []
@@ -120,16 +121,17 @@ def tile_mix_atom_tm_silu_kernel(tc, x8, w8, x4_words, x4_scales, w4_words, w4_s
 
         opened = set()
 
-        def fp4(i):
+        def fp4(i, passes):
             tiles, n0, width = layout[i]
-            words, c0 = (w4w_left, n0) if n0 < HALF else (w4w_right, n0 - HALF)
             for s, t in enumerate(tiles):
-                for a in range(G4):
+                for a in passes:
+                    x_words = x4w_last[:] if a == G4 - 1 else x4w[:, a, :]
+                    w_words = w4w_last[:] if a == G4 - 1 else w4w[:, a, :]
                     nc.tensor.matmul_mx(
                         out=acc[i][:, s, :],
-                        lhsT=x4w[:, a, 2 * P * t : 2 * P * (t + 1)].bitcast(FP4X4),
+                        lhsT=x_words[:, 2 * P * t : 2 * P * (t + 1)].bitcast(FP4X4),
                         lhsT_scale=x4s[:, a, P * t : P * (t + 1)],
-                        rhs=words[:, a, 2 * c0 : 2 * (c0 + width)].bitcast(FP4X4),
+                        rhs=w_words[:, 2 * n0 : 2 * (n0 + width)].bitcast(FP4X4),
                         rhs_scale=w4s[:, a, n0 : n0 + width],
                         start=i not in opened,
                         stop=False,
@@ -178,6 +180,14 @@ def tile_mix_atom_tm_silu_kernel(tc, x8, w8, x4_words, x4_scales, w4_words, w4_s
             row = bias[:, n0 : n0 + width].rearrange("p (o n) -> p o n", o=1)
             nc.vector.tensor_add(out=z[:], in0=acc[i][:], in1=row.to_broadcast([P, len(tiles), width]))
 
+        def add_half(i, h):
+            tiles, n0, width = layout[i]
+            if h == 0:
+                z = sb.tile([P, 1, width], F32, name="z%d" % i)
+                summed[i] = z
+            cols = slice(h * QUARTER, (h + 1) * QUARTER)
+            nc.vector.tensor_add(out=summed[i][:, 0, cols], in0=acc[i][:, 0, cols], in1=bias[:, cols])
+
         def silu_store(i):
             tiles, n0, width = layout[i]
             y = sb.tile([P, len(tiles), width], F32, name="y%d" % i)
@@ -208,16 +218,16 @@ def tile_mix_atom_tm_silu_kernel(tc, x8, w8, x4_words, x4_scales, w4_words, w4_s
             queue.dma_start(out=out[P * t : P * (t + 1), n0 : n0 + width], in_=y[:])
 
         open_banks(0, 6)
-        for i in range(3):
-            fp4(i)
+        for i in range(5):
+            fp4(i, (0, 1))
         prep("x0")
         copy_bias()
         open_banks(6, 8)
         prep("w0a")
         for i in range(4):
             fp8(i, "x0", "w0a", 0, False)
-        for i in range(3, 4):
-            fp4(i)
+        for i in range(5, 8):
+            fp4(i, (0, 1))
         prep("w1a")
         vcopy("x1", 0, P // 2)
         scopy("x1", P // 2, P)
@@ -228,37 +238,39 @@ def tile_mix_atom_tm_silu_kernel(tc, x8, w8, x4_words, x4_scales, w4_words, w4_s
         for t in range(1, TT):
             quant("x1", P * t, P * (t + 1))
         for t in range(TT):
+            fp4(t, (2,))
             fp8(t, "x1", "w1a", 0, True)
         for i in range(4, 8):
-            fp4(i)
+            fp4(i, (2,))
         for i in range(2):
             add(i)
             silu_store(i)
         add(2)
         vcopy("w0b", 0, 256)
         scopy("w0b", 256, 512)
-        add(3)
+        add_half(3, 0)
         quant("w0b", 0, 256)
         for i in range(4, 6):
             fp8(i, "x0", "w0b", layout[i][1] - HALF, False)
-        vcopy("w1c", 0, 128)
-        scopy("w1c", 128, 256)
+        vcopy("w1c", 0, 192)
+        scopy("w1c", 192, 256)
         silu_store(2)
-        quant("w0b", 256, 512)
+        add_half(3, 1)
         quant("w1c")
         fp8(4, "x1", "w1c", 0, True)
         fp8(5, "x1", "w1c", 0, True)
+        quant("w0b", 256, 512)
         for i in range(6, 8):
             fp8(i, "x0", "w0b", layout[i][1] - HALF, False)
-        vcopy("w1d", 0, 128)
-        scopy("w1d", 128, 256)
         silu_store(3)
+        vcopy("w1d", 0, 192)
+        scopy("w1d", 192, 256)
         add_tile(4, 0)
+        silu_tile(4, 0)
         add_tile(4, 1)
         quant("w1d")
         fp8(6, "x1", "w1d", 0, True)
         fp8(7, "x1", "w1d", 0, True)
-        silu_tile(4, 0)
         silu_tile(4, 1)
         for i in range(5, 8):
             finish_tile(i, 0, nc.sync)

@@ -83,13 +83,11 @@ def tile_mix_atom_tm_silu_kernel(tc, x8, w8, x4_words, x4_scales, w4_words, w4_s
         nc.sync.dma_start(out=x4w[:], in_=x4_words[0 : G4 - 1].rearrange("a p n -> p a n"))
         for r in range(4):
             nc.sync.dma_start(out=x4s[r:P:32, :, :].bitcast(I32), in_=xs_v[r].bitcast(I32))
-        nc.sync.dma_start(out=raw["x0"][:], in_=sources["x0"])
         nc.sync.dma_start(out=w4w[:], in_=w4_words[0 : G4 - 1].rearrange("a p n -> p a n"))
         for r in range(4):
             nc.sync.dma_start(out=w4s[r:P:32, :, :].bitcast(I32), in_=ws_v[r].bitcast(I32))
         for key, src in sources.items():
-            if key != "x0":
-                nc.sync.dma_start(out=raw[key][:], in_=src)
+            nc.sync.dma_start(out=raw[key][:], in_=src)
             if key == "x1":
                 nc.sync.dma_start(out=x4w_last[:], in_=x4_words[G4 - 1])
                 nc.sync.dma_start(out=w4w_last[:], in_=w4_words[G4 - 1])
@@ -218,7 +216,7 @@ def tile_mix_atom_tm_silu_kernel(tc, x8, w8, x4_words, x4_scales, w4_words, w4_s
             queue.dma_start(out=out[P * t : P * (t + 1), n0 : n0 + width], in_=y[:])
 
         open_banks(0, 6)
-        for i in range(5):
+        for i in range(6):
             fp4(i, (0, 1))
         prep("x0")
         copy_bias()
@@ -226,7 +224,7 @@ def tile_mix_atom_tm_silu_kernel(tc, x8, w8, x4_words, x4_scales, w4_words, w4_s
         prep("w0a")
         for i in range(4):
             fp8(i, "x0", "w0a", 0, False)
-        for i in range(5, 8):
+        for i in range(6, 8):
             fp4(i, (0, 1))
         prep("w1a")
         vcopy("x1", 0, P // 2)
@@ -263,8 +261,8 @@ def tile_mix_atom_tm_silu_kernel(tc, x8, w8, x4_words, x4_scales, w4_words, w4_s
         for i in range(6, 8):
             fp8(i, "x0", "w0b", layout[i][1] - HALF, False)
         silu_store(3)
-        vcopy("w1d", 0, 192)
-        scopy("w1d", 192, 256)
+        vcopy("w1d", 0, 160)
+        scopy("w1d", 160, 256)
         add_tile(4, 0)
         silu_tile(4, 0)
         add_tile(4, 1)

@@ -74,20 +74,21 @@ def tile_mix_atom_tm_silu_kernel(tc, x8, w8, x4_words, x4_scales, w4_words, w4_s
             codes[key] = sb.tile([P, width], U32, name="codes_" + key, align_bytes=64)
             scales[key] = sb.tile([P, width], U8, name="scales_" + key, align_bytes=64)
 
-        nc.vector.memset(x4s[:].rearrange("p a n -> p (a n)").bitcast(I32), 0)
+        nc.gpsimd.memset(x4s[:].rearrange("p a n -> p (a n)").bitcast(I32), 0)
         nc.vector.memset(w4s[:].rearrange("p a n -> p (a n)").bitcast(I32), 0)
         nc.vector.memset(warm_in[:], 0.0)
 
-        nc.gpsimd.dma_start(out=b_col[:], in_=b.rearrange("(p c) -> p c", p=P))
         make_identity(nc, ident[:])
-        nc.sync.dma_start(out=x4w[:], in_=x4_words[0 : G4 - 1].rearrange("a p n -> p a n"))
+        nc.sync.dma_start(out=w4w[:], in_=w4_words[0 : G4 - 1].rearrange("a p n -> p a n"))
+        nc.sync.dma_start(out=b_col[:], in_=b.rearrange("(p c) -> p c", p=P))
         for r in range(4):
             nc.sync.dma_start(out=x4s[r:P:32, :, :].bitcast(I32), in_=xs_v[r].bitcast(I32))
-        nc.sync.dma_start(out=w4w[:], in_=w4_words[0 : G4 - 1].rearrange("a p n -> p a n"))
-        for r in range(4):
-            nc.sync.dma_start(out=w4s[r:P:32, :, :].bitcast(I32), in_=ws_v[r].bitcast(I32))
+        nc.sync.dma_start(out=x4w[:], in_=x4_words[0 : G4 - 1].rearrange("a p n -> p a n"))
         for key, src in sources.items():
             nc.sync.dma_start(out=raw[key][:], in_=src)
+            if key == "x0":
+                for r in range(4):
+                    nc.sync.dma_start(out=w4s[r:P:32, :, :].bitcast(I32), in_=ws_v[r].bitcast(I32))
             if key == "x1":
                 nc.sync.dma_start(out=x4w_last[:], in_=x4_words[G4 - 1])
                 nc.sync.dma_start(out=w4w_last[:], in_=w4_words[G4 - 1])
@@ -215,12 +216,11 @@ def tile_mix_atom_tm_silu_kernel(tc, x8, w8, x4_words, x4_scales, w4_words, w4_s
             nc.scalar.activation(out=y[:], in_=z[:], func=SILU)
             queue.dma_start(out=out[P * t : P * (t + 1), n0 : n0 + width], in_=y[:])
 
-        open_banks(0, 6)
+        copy_bias()
+        open_banks(0, 8)
         for i in range(6):
             fp4(i, (0, 1))
         prep("x0")
-        copy_bias()
-        open_banks(6, 8)
         prep("w0a")
         for i in range(4):
             fp8(i, "x0", "w0a", 0, False)

@@ -40,15 +40,15 @@ def tile_mix_atom_tm_silu_kernel(tc, x8, w8, x4_words, x4_scales, w4_words, w4_s
         psum = ctx.enter_context(tc.psum_pool(name="psum", bufs=1))
         ctx.enter_context(tc.manual_schedule())
 
-        x4w = sb.tile([P, G4 - 1, 2 * T], U8, name="x4w", align_bytes=64)
-        w4w = sb.tile([P, G4 - 1, 2 * N], U8, name="w4w", align_bytes=64)
-        x4w_last = sb.tile([P, 2 * T], U8, name="x4w_last", align_bytes=64)
-        w4w_last = sb.tile([P, 2 * N], U8, name="w4w_last", align_bytes=64)
-        x4s = sb.tile([P, G4, T], U8, name="x4s", align_bytes=64)
-        w4s = sb.tile([P, G4, N], U8, name="w4s", align_bytes=64)
+        x4w = sb.tile([P, G4 - 1, 2 * T], U8, name="x4w", align_bytes=256)
+        w4w = sb.tile([P, G4 - 1, 2 * N], U8, name="w4w", align_bytes=256)
+        x4w_last = sb.tile([P, 2 * T], U8, name="x4w_last", align_bytes=256)
+        w4w_last = sb.tile([P, 2 * N], U8, name="w4w_last", align_bytes=256)
+        x4s = sb.tile([P, G4, T], U8, name="x4s", align_bytes=256)
+        w4s = sb.tile([P, G4, N], U8, name="w4s", align_bytes=256)
         b_col = sb.tile([P, N // P], F32, name="b_col")
         ident = sb.tile([P, P], F32, name="ident")
-        bias = sb.tile([P, N], F32, name="bias")
+        bias = sb.tile([P, N], F32, name="bias", align_bytes=256)
         warm_in = sb.tile([P, 1], F32, name="warm_in")
         warm_out = sb.tile([P, 1], F32, name="warm_out")
 
@@ -69,10 +69,10 @@ def tile_mix_atom_tm_silu_kernel(tc, x8, w8, x4_words, x4_scales, w4_words, w4_s
         raw, grouped, codes, scales = {}, {}, {}, {}
         for key, src in sources.items():
             width = src.shape[2]
-            raw[key] = sb.tile([P, PACK, width], F32, name="raw_" + key)
-            grouped[key] = sb.tile([P, width, PACK], BF16, name="grouped_" + key, align_bytes=64)
-            codes[key] = sb.tile([P, width], U32, name="codes_" + key, align_bytes=64)
-            scales[key] = sb.tile([P, width], U8, name="scales_" + key, align_bytes=64)
+            raw[key] = sb.tile([P, PACK, width], F32, name="raw_" + key, align_bytes=256)
+            grouped[key] = sb.tile([P, width, PACK], BF16, name="grouped_" + key, align_bytes=256)
+            codes[key] = sb.tile([P, width], U32, name="codes_" + key, align_bytes=256)
+            scales[key] = sb.tile([P, width], U8, name="scales_" + key, align_bytes=256)
 
         nc.gpsimd.memset(x4s[:].rearrange("p a n -> p (a n)").bitcast(I32), 0)
         nc.vector.memset(w4s[:].rearrange("p a n -> p (a n)").bitcast(I32), 0)
@@ -174,7 +174,7 @@ def tile_mix_atom_tm_silu_kernel(tc, x8, w8, x4_words, x4_scales, w4_words, w4_s
 
         def add(i):
             tiles, n0, width = layout[i]
-            z = sb.tile([P, len(tiles), width], F32, name="z%d" % i)
+            z = sb.tile([P, len(tiles), width], F32, name="z%d" % i, align_bytes=256)
             summed[i] = z
             row = bias[:, n0 : n0 + width].rearrange("p (o n) -> p o n", o=1)
             nc.vector.tensor_add(out=z[:], in0=acc[i][:], in1=row.to_broadcast([P, len(tiles), width]))
@@ -182,36 +182,36 @@ def tile_mix_atom_tm_silu_kernel(tc, x8, w8, x4_words, x4_scales, w4_words, w4_s
         def add_half(i, h):
             tiles, n0, width = layout[i]
             if h == 0:
-                z = sb.tile([P, 1, width], F32, name="z%d" % i)
+                z = sb.tile([P, 1, width], F32, name="z%d" % i, align_bytes=256)
                 summed[i] = z
             cols = slice(h * QUARTER, (h + 1) * QUARTER)
             nc.vector.tensor_add(out=summed[i][:, 0, cols], in0=acc[i][:, 0, cols], in1=bias[:, cols])
 
         def silu_store(i):
             tiles, n0, width = layout[i]
-            y = sb.tile([P, len(tiles), width], F32, name="y%d" % i)
+            y = sb.tile([P, len(tiles), width], F32, name="y%d" % i, align_bytes=256)
             nc.scalar.activation(out=y[:], in_=summed[i][:], func=SILU)
             rows = out[P * tiles[0] : P * (tiles[-1] + 1), n0 : n0 + width]
             nc.sync.dma_start(out=rows.rearrange("(s p) n -> p s n", p=P), in_=y[:])
 
         def add_tile(i, s):
             tiles, n0, width = layout[i]
-            z = sb.tile([P, width], F32, name="z_tile%d_%d" % (i, s))
+            z = sb.tile([P, width], F32, name="z_tile%d_%d" % (i, s), align_bytes=256)
             summed[(i, s)] = z
             nc.vector.tensor_add(out=z[:], in0=acc[i][:, s, :], in1=bias[:, n0 : n0 + width])
 
         def silu_tile(i, s):
             tiles, n0, width = layout[i]
             t = tiles[s]
-            y = sb.tile([P, width], F32, name="y_tile%d_%d" % (i, s))
+            y = sb.tile([P, width], F32, name="y_tile%d_%d" % (i, s), align_bytes=256)
             nc.scalar.activation(out=y[:], in_=summed[(i, s)][:], func=SILU)
             nc.sync.dma_start(out=out[P * t : P * (t + 1), n0 : n0 + width], in_=y[:])
 
         def finish_tile(i, s, queue):
             tiles, n0, width = layout[i]
             t = tiles[s]
-            z = sb.tile([P, width], F32, name="z_tile%d_%d" % (i, s))
-            y = sb.tile([P, width], F32, name="y_tile%d_%d" % (i, s))
+            z = sb.tile([P, width], F32, name="z_tile%d_%d" % (i, s), align_bytes=256)
+            y = sb.tile([P, width], F32, name="y_tile%d_%d" % (i, s), align_bytes=256)
             nc.vector.tensor_add(out=z[:], in0=acc[i][:, s, :], in1=bias[:, n0 : n0 + width])
             nc.scalar.activation(out=y[:], in_=z[:], func=SILU)
             queue.dma_start(out=out[P * t : P * (t + 1), n0 : n0 + width], in_=y[:])

@@ -80,10 +80,10 @@ def tile_mix_atom_tm_silu_kernel(tc, x8, w8, x4_words, x4_scales, w4_words, w4_s
 
         make_identity(nc, ident[:])
         nc.sync.dma_start(out=w4w[:], in_=w4_words[0 : G4 - 1].rearrange("a p n -> p a n"))
+        nc.sync.dma_start(out=x4w[:], in_=x4_words[0 : G4 - 1].rearrange("a p n -> p a n"))
         nc.sync.dma_start(out=b_col[:], in_=b.rearrange("(p c) -> p c", p=P))
         for r in range(4):
             nc.sync.dma_start(out=x4s[r:P:32, :, :].bitcast(I32), in_=xs_v[r].bitcast(I32))
-        nc.sync.dma_start(out=x4w[:], in_=x4_words[0 : G4 - 1].rearrange("a p n -> p a n"))
         for key, src in sources.items():
             nc.sync.dma_start(out=raw[key][:], in_=src)
             if key == "x0":

@@ -157,6 +157,16 @@ def tile_mix_atom_tm_silu_kernel(tc, x8, w8, x4_words, x4_scales, w4_words, w4_s
         def scopy(key, c0, c1):
             interleave(nc.scalar.copy, grouped[key], raw[key], c0, c1)
 
+        def gcopy(key, c0, c1):
+            nc.gpsimd.tensor_scalar(
+                out=grouped[key][:, c0:c1, :].rearrange("p (c i) j -> p c j i", i=4),
+                in0=raw[key][:, :, c0:c1].rearrange("p j (c i) -> p c j i", i=4),
+                scalar1=1.0,
+                scalar2=0.0,
+                op0=mybir.AluOpType.mult,
+                op1=mybir.AluOpType.add,
+            )
+
         def quant(key, c0=0, c1=None):
             nc.vector.quantize_mx(
                 out=codes[key][:, c0:c1].bitcast(FP8X4),
@@ -244,31 +254,31 @@ def tile_mix_atom_tm_silu_kernel(tc, x8, w8, x4_words, x4_scales, w4_words, w4_s
             add(i)
             silu_store(i)
         add(2)
+        gcopy("w0b", 416, 512)
+        scopy("w0b", 256, 416)
+        add(3)
         vcopy("w0b", 0, 256)
-        scopy("w0b", 256, 512)
-        add_half(3, 0)
+        vcopy("w1c", 0, 128)
+        scopy("w1c", 128, 256)
+        silu_store(2)
         quant("w0b", 0, 256)
         for i in range(4, 6):
             fp8(i, "x0", "w0b", layout[i][1] - HALF, False)
-        vcopy("w1c", 0, 192)
-        scopy("w1c", 192, 256)
-        silu_store(2)
-        add_half(3, 1)
         quant("w1c")
         fp8(4, "x1", "w1c", 0, True)
         fp8(5, "x1", "w1c", 0, True)
         quant("w0b", 256, 512)
         for i in range(6, 8):
             fp8(i, "x0", "w0b", layout[i][1] - HALF, False)
+        vcopy("w1d", 0, 128)
+        scopy("w1d", 128, 256)
         silu_store(3)
-        vcopy("w1d", 0, 160)
-        scopy("w1d", 160, 256)
         add_tile(4, 0)
-        silu_tile(4, 0)
-        add_tile(4, 1)
         quant("w1d")
         fp8(6, "x1", "w1d", 0, True)
         fp8(7, "x1", "w1d", 0, True)
+        silu_tile(4, 0)
+        add_tile(4, 1)
         silu_tile(4, 1)
         for i in range(5, 8):
             finish_tile(i, 0, nc.sync)

@@ -234,8 +234,7 @@ def tile_mix_atom_tm_silu_kernel(tc, x8, w8, x4_words, x4_scales, w4_words, w4_s
         prep("w0a")
         for i in range(4):
             fp8(i, "x0", "w0a", 0, False)
-        for i in range(6, 8):
-            fp4(i, (0, 1))
+        fp4(6, (0, 1))
         prep("w1a")
         vcopy("x1", 0, P // 2)
         scopy("x1", P // 2, P)
@@ -248,8 +247,9 @@ def tile_mix_atom_tm_silu_kernel(tc, x8, w8, x4_words, x4_scales, w4_words, w4_s
         for t in range(TT):
             fp4(t, (2,))
             fp8(t, "x1", "w1a", 0, True)
-        for i in range(4, 8):
+        for i in range(4, 7):
             fp4(i, (2,))
+        fp4(7, (0, 1, 2))
         for i in range(2):
             add(i)
             silu_store(i)
@@ -262,11 +262,10 @@ def tile_mix_atom_tm_silu_kernel(tc, x8, w8, x4_words, x4_scales, w4_words, w4_s
         scopy("w1c", 128, 256)
         silu_store(2)
         quant("w0b", 0, 256)
+        quant("w1c")
         for i in range(4, 6):
             fp8(i, "x0", "w0b", layout[i][1] - HALF, False)
-        quant("w1c")
-        fp8(4, "x1", "w1c", 0, True)
-        fp8(5, "x1", "w1c", 0, True)
+            fp8(i, "x1", "w1c", 0, True)
         quant("w0b", 256, 512)
         for i in range(6, 8):
             fp8(i, "x0", "w0b", layout[i][1] - HALF, False)

@@ -250,35 +250,31 @@ def tile_mix_atom_tm_silu_kernel(tc, x8, w8, x4_words, x4_scales, w4_words, w4_s
         for i in range(4, 7):
             fp4(i, (2,))
         fp4(7, (0, 1, 2))
-        for i in range(2):
-            add(i)
-            silu_store(i)
+        add(0)
+        silu_store(0)
+        add(1)
         add(2)
         gcopy("w0b", 416, 512)
-        scopy("w0b", 256, 416)
+        scopy("w0b", 0, 256)
         add(3)
-        vcopy("w0b", 0, 256)
+        vcopy("w0b", 256, 416)
         vcopy("w1c", 0, 128)
         scopy("w1c", 128, 256)
-        silu_store(2)
+        silu_store(1)
         quant("w0b", 0, 256)
         quant("w1c")
         for i in range(4, 6):
             fp8(i, "x0", "w0b", layout[i][1] - HALF, False)
             fp8(i, "x1", "w1c", 0, True)
+        vcopy("w1d", 0, 160)
+        scopy("w1d", 160, 256)
         quant("w0b", 256, 512)
+        quant("w1d")
         for i in range(6, 8):
             fp8(i, "x0", "w0b", layout[i][1] - HALF, False)
-        vcopy("w1d", 0, 128)
-        scopy("w1d", 128, 256)
+            fp8(i, "x1", "w1d", 0, True)
+        silu_store(2)
         silu_store(3)
-        add_tile(4, 0)
-        quant("w1d")
-        fp8(6, "x1", "w1d", 0, True)
-        fp8(7, "x1", "w1d", 0, True)
-        silu_tile(4, 0)
-        add_tile(4, 1)
-        silu_tile(4, 1)
-        for i in range(5, 8):
+        for i in range(4, 8):
             finish_tile(i, 0, nc.sync)
             finish_tile(i, 1, nc.sync)

@@ -254,10 +254,10 @@ def tile_mix_atom_tm_silu_kernel(tc, x8, w8, x4_words, x4_scales, w4_words, w4_s
         silu_store(0)
         add(1)
         add(2)
-        gcopy("w0b", 416, 512)
+        gcopy("w0b", 320, 512)
         scopy("w0b", 0, 256)
         add(3)
-        vcopy("w0b", 256, 416)
+        vcopy("w0b", 256, 320)
         vcopy("w1c", 0, 128)
         scopy("w1c", 128, 256)
         silu_store(1)

from contextlib import ExitStack

import concourse.mybir as mybir
from concourse.masks import make_identity

F32 = mybir.dt.float32
BF16 = mybir.dt.bfloat16
I32 = mybir.dt.int32
U32 = mybir.dt.uint32
U8 = mybir.dt.uint8
FP8X4 = mybir.dt.float8_e4m3fn_x4
FP4X4 = mybir.dt.float4_e2m1fn_x4
SILU = mybir.ActivationFunctionType.Silu

P = 128
PACK = 4
K_PASS = P * PACK
T, N = 512, 1024
K8, K4 = 1024, 1536
G8, G4 = K8 // K_PASS, K4 // K_PASS
TT = T // P
BANK = 512
HALF = N // 2
QUARTER = N // 4

FLOPS = 2 * (K8 + K4) * T * N


def interleave(copy, grouped, raw, c0, c1):
    copy(
        out=grouped[:, c0:c1, :].rearrange("p (c i) j -> p c j i", i=4),
        in_=raw[:, :, c0:c1].rearrange("p j (c i) -> p c j i", i=4),
    )


def tile_mix_atom_tm_silu_kernel(tc, x8, w8, x4_words, x4_scales, w4_words, w4_scales, b, out):
    nc = tc.nc
    with ExitStack() as ctx:
        sb = ctx.enter_context(tc.tile_pool(name="sb", bufs=1))
        psum = ctx.enter_context(tc.psum_pool(name="psum", bufs=1))
        ctx.enter_context(tc.manual_schedule())

        x4w = sb.tile([P, G4 - 1, 2 * T], U8, name="x4w", align_bytes=256)
        w4w = sb.tile([P, G4 - 1, 2 * N], U8, name="w4w", align_bytes=256)
        x4w_last = sb.tile([P, 2 * T], U8, name="x4w_last", align_bytes=256)
        w4w_last = sb.tile([P, 2 * N], U8, name="w4w_last", align_bytes=256)
        x4s = sb.tile([P, G4, T], U8, name="x4s", align_bytes=256)
        w4s = sb.tile([P, G4, N], U8, name="w4s", align_bytes=256)
        b_col = sb.tile([P, N // P], F32, name="b_col")
        ident = sb.tile([P, P], F32, name="ident")
        bias = sb.tile([P, N], F32, name="bias", align_bytes=256)
        warm_in = sb.tile([P, 1], F32, name="warm_in")
        warm_out = sb.tile([P, 1], F32, name="warm_out")

        x8_v = x8.rearrange("(g p j) t -> g p j t", p=P, j=PACK)
        w8_v = w8.rearrange("(g p j) n -> g p j n", p=P, j=PACK)
        ws_v = w4_scales.rearrange("a (q r) n -> r q a n", r=4)
        xs_v = x4_scales.rearrange("a (q r) n -> r q a n", r=4)

        sources = {
            "x0": x8_v[0],
            "w0a": w8_v[0][:, :, 0:HALF],
            "w1a": w8_v[1][:, :, 0:HALF],
            "x1": x8_v[1],
            "w0b": w8_v[0][:, :, HALF:N],
            "w1c": w8_v[1][:, :, HALF : HALF + QUARTER],
            "w1d": w8_v[1][:, :, HALF + QUARTER : N],
        }
        raw, grouped, codes, scales = {}, {}, {}, {}
        for key, src in sources.items():
            width = src.shape[2]
            raw[key] = sb.tile([P, PACK, width], F32, name="raw_" + key, align_bytes=256)
            grouped[key] = sb.tile([P, width, PACK], BF16, name="grouped_" + key, align_bytes=256)
            codes[key] = sb.tile([P, width], U32, name="codes_" + key, align_bytes=256)
            scales[key] = sb.tile([P, width], U8, name="scales_" + key, align_bytes=256)

        nc.gpsimd.memset(x4s[:].rearrange("p a n -> p (a n)").bitcast(I32), 0)
        nc.vector.memset(w4s[:].rearrange("p a n -> p (a n)").bitcast(I32), 0)
        nc.vector.memset(warm_in[:], 0.0)

        make_identity(nc, ident[:])
        nc.sync.dma_start(out=w4w[:], in_=w4_words[0 : G4 - 1].rearrange("a p n -> p a n"))
        nc.sync.dma_start(out=x4w[:], in_=x4_words[0 : G4 - 1].rearrange("a p n -> p a n"))
        nc.sync.dma_start(out=b_col[:], in_=b.rearrange("(p c) -> p c", p=P))
        for r in range(4):
            nc.sync.dma_start(out=x4s[r:P:32, :, :].bitcast(I32), in_=xs_v[r].bitcast(I32))
        for key, src in sources.items():
            nc.sync.dma_start(out=raw[key][:], in_=src)
            if key == "x0":
                for r in range(4):
                    nc.sync.dma_start(out=w4s[r:P:32, :, :].bitcast(I32), in_=ws_v[r].bitcast(I32))
            if key == "x1":
                nc.sync.dma_start(out=x4w_last[:], in_=x4_words[G4 - 1])
                nc.sync.dma_start(out=w4w_last[:], in_=w4_words[G4 - 1])
        nc.scalar.activation(out=warm_out[:], in_=warm_in[:], func=SILU)

        spread = []
        for h in range(2):
            bp = psum.tile([P, 4, P], F32, name="bp%d" % h, tag="bank%d" % (6 + h))
            spread.append(bp)
            for c in range(4):
                nc.tensor.transpose(bp[:, c, :], b_col[:, 4 * h + c : 4 * h + c + 1].to_broadcast([P, P]), ident[:])

        def copy_bias():
            for h, copy in enumerate([nc.vector.tensor_copy, nc.scalar.copy]):
                copy(
                    out=bias[:].rearrange("q (p c) -> q p c", c=8)[:, :, 4 * h : 4 * h + 4],
                    in_=spread[h][:].rearrange("q c p -> q p c"),
                )

        layout = [([t], 0, HALF) for t in range(TT)]
        layout = layout + [([t, t + 1], n0, QUARTER) for n0 in (HALF, HALF + QUARTER) for t in (0, 2)]
        acc = []

        def open_banks(first, last):
            for i in range(first, last):
                tiles, n0, width = layout[i]
                bank_tile = psum.tile([P, len(tiles), width], F32, name="acc%d" % i, tag="bank%d" % i)
                acc.append(bank_tile)

        opened = set()

        def fp4(i, passes):
            tiles, n0, width = layout[i]
            for s, t in enumerate(tiles):
                for a in passes:
                    x_words = x4w_last[:] if a == G4 - 1 else x4w[:, a, :]
                    w_words = w4w_last[:] if a == G4 - 1 else w4w[:, a, :]
                    nc.tensor.matmul_mx(
                        out=acc[i][:, s, :],
                        lhsT=x_words[:, 2 * P * t : 2 * P * (t + 1)].bitcast(FP4X4),
                        lhsT_scale=x4s[:, a, P * t : P * (t + 1)],
                        rhs=w_words[:, 2 * n0 : 2 * (n0 + width)].bitcast(FP4X4),
                        rhs_scale=w4s[:, a, n0 : n0 + width],
                        start=i not in opened,
                        stop=False,
                    )
                    opened.add(i)

        def fp8(i, xkey, wkey, c0, last):
            tiles, n0, width = layout[i]
            for s, t in enumerate(tiles):
                nc.tensor.matmul_mx(
                    out=acc[i][:, s, :],
                    lhsT=codes[xkey][:, P * t : P * (t + 1)].bitcast(FP8X4),
                    lhsT_scale=scales[xkey][:, P * t : P * (t + 1)],
                    rhs=codes[wkey][:, c0 : c0 + width].bitcast(FP8X4),
                    rhs_scale=scales[wkey][:, c0 : c0 + width],
                    start=i not in opened,
                    stop=last and s == len(tiles) - 1,
                )
                opened.add(i)

        def vcopy(key, c0, c1):
            interleave(nc.vector.tensor_copy, grouped[key], raw[key], c0, c1)

        def scopy(key, c0, c1):
            interleave(nc.scalar.copy, grouped[key], raw[key], c0, c1)

        def gcopy(key, c0, c1):
            nc.gpsimd.tensor_scalar(
                out=grouped[key][:, c0:c1, :].rearrange("p (c i) j -> p c j i", i=4),
                in0=raw[key][:, :, c0:c1].rearrange("p j (c i) -> p c j i", i=4),
                scalar1=1.0,
                scalar2=0.0,
                op0=mybir.AluOpType.mult,
                op1=mybir.AluOpType.add,
            )

        def quant(key, c0=0, c1=None):
            nc.vector.quantize_mx(
                out=codes[key][:, c0:c1].bitcast(FP8X4),
                scales=scales[key][:, c0:c1],
                in_=grouped[key][:, c0:c1, :].rearrange("p n j -> p (n j)"),
            )

        def prep(key):
            vcopy(key, 0, QUARTER)
            scopy(key, QUARTER, HALF)
            quant(key, 0, QUARTER)
            quant(key, QUARTER, HALF)

        summed = {}

        def add(i):
            tiles, n0, width = layout[i]
            z = sb.tile([P, len(tiles), width], F32, name="z%d" % i, align_bytes=256)
            summed[i] = z
            row = bias[:, n0 : n0 + width].rearrange("p (o n) -> p o n", o=1)
            nc.vector.tensor_add(out=z[:], in0=acc[i][:], in1=row.to_broadcast([P, len(tiles), width]))

        def add_half(i, h):
            tiles, n0, width = layout[i]
            if h == 0:
                z = sb.tile([P, 1, width], F32, name="z%d" % i, align_bytes=256)
                summed[i] = z
            cols = slice(h * QUARTER, (h + 1) * QUARTER)
            nc.vector.tensor_add(out=summed[i][:, 0, cols], in0=acc[i][:, 0, cols], in1=bias[:, cols])

        def silu_store(i):
            tiles, n0, width = layout[i]
            y = sb.tile([P, len(tiles), width], F32, name="y%d" % i, align_bytes=256)
            nc.scalar.activation(out=y[:], in_=summed[i][:], func=SILU)
            rows = out[P * tiles[0] : P * (tiles[-1] + 1), n0 : n0 + width]
            nc.sync.dma_start(out=rows.rearrange("(s p) n -> p s n", p=P), in_=y[:])

        def add_tile(i, s):
            tiles, n0, width = layout[i]
            z = sb.tile([P, width], F32, name="z_tile%d_%d" % (i, s), align_bytes=256)
            summed[(i, s)] = z
            nc.vector.tensor_add(out=z[:], in0=acc[i][:, s, :], in1=bias[:, n0 : n0 + width])

        def silu_tile(i, s):
            tiles, n0, width = layout[i]
            t = tiles[s]
            y = sb.tile([P, width], F32, name="y_tile%d_%d" % (i, s), align_bytes=256)
            nc.scalar.activation(out=y[:], in_=summed[(i, s)][:], func=SILU)
            nc.sync.dma_start(out=out[P * t : P * (t + 1), n0 : n0 + width], in_=y[:])

        def finish_tile(i, s, queue):
            tiles, n0, width = layout[i]
            t = tiles[s]
            z = sb.tile([P, width], F32, name="z_tile%d_%d" % (i, s), align_bytes=256)
            y = sb.tile([P, width], F32, name="y_tile%d_%d" % (i, s), align_bytes=256)
            nc.vector.tensor_add(out=z[:], in0=acc[i][:, s, :], in1=bias[:, n0 : n0 + width])
            nc.scalar.activation(out=y[:], in_=z[:], func=SILU)
            queue.dma_start(out=out[P * t : P * (t + 1), n0 : n0 + width], in_=y[:])

        copy_bias()
        open_banks(0, 8)
        for i in range(6):
            fp4(i, (0, 1))
        prep("x0")
        prep("w0a")
        for i in range(4):
            fp8(i, "x0", "w0a", 0, False)
        fp4(6, (0, 1))
        prep("w1a")
        vcopy("x1", 0, P // 2)
        scopy("x1", P // 2, P)
        vcopy("x1", P, 2 * P)
        scopy("x1", 2 * P, 3 * P)
        quant("x1", 0, P)
        vcopy("x1", 3 * P, 4 * P)
        for t in range(1, TT):
            quant("x1", P * t, P * (t + 1))
        for t in range(TT):
            fp4(t, (2,))
            fp8(t, "x1", "w1a", 0, True)
        for i in range(4, 7):
            fp4(i, (2,))
        fp4(7, (0, 1, 2))
        add(0)
        silu_store(0)
        add(1)
        add(2)
        gcopy("w0b", 320, 512)
        scopy("w0b", 0, 256)
        add(3)
        vcopy("w0b", 256, 320)
        vcopy("w1c", 0, 128)
        scopy("w1c", 128, 256)
        silu_store(1)
        quant("w0b", 0, 256)
        quant("w1c")
        for i in range(4, 6):
            fp8(i, "x0", "w0b", layout[i][1] - HALF, False)
            fp8(i, "x1", "w1c", 0, True)
        vcopy("w1d", 0, 160)
        scopy("w1d", 160, 256)
        quant("w0b", 256, 512)
        quant("w1d")
        for i in range(6, 8):
            fp8(i, "x0", "w0b", layout[i][1] - HALF, False)
            fp8(i, "x1", "w1d", 0, True)
        silu_store(2)
        silu_store(3)
        for i in range(4, 8):
            finish_tile(i, 0, nc.sync)
            finish_tile(i, 1, nc.sync)
